import numpy as np
import ml_dtypes


def mxq(x, axis, fmt="e4m3"):
    dtype, down = {"e4m3": (ml_dtypes.float8_e4m3fn, 7), "e5m2": (ml_dtypes.float8_e5m2, 14)}[fmt]
    v = np.moveaxis(np.asarray(x, np.float32).astype(ml_dtypes.bfloat16).astype(np.float64), axis, -1)
    blocks = v.reshape(v.shape[:-1] + (-1, 32))
    amax = np.abs(blocks).max(-1, keepdims=True)
    byte = np.maximum(np.where(amax > 0, np.frexp(amax)[1] - 1 + 127, 0) - down, 1)
    scale = np.exp2(byte - 127.0)
    codes = (blocks / scale).astype(np.float32).astype(dtype).astype(np.float64)
    return np.moveaxis((codes * scale).reshape(v.shape), -1, axis)


WIDE = False


def mx_kscale(k):
    if not WIDE:
        return np.ones(k)
    levels = np.array([10, -10, 5, -5, 0])
    if k % 512:
        return np.exp2(np.random.permutation(np.resize(levels, k // 32))).repeat(32)
    a = np.empty((k // 512, 16))
    for p in range(k // 512):
        a[p, :8] = np.random.permutation(np.resize(levels, 8))
        for g in range(8):
            far = levels[np.abs(levels - a[p, g]) >= 10]
            a[p, g + 8] = far[np.random.randint(len(far))]
    return np.exp2(a.ravel()).repeat(32)


BF16 = ml_dtypes.bfloat16


def bf(x):
    return np.asarray(x, np.float32).astype(BF16)


def f64(x):
    return np.asarray(x).astype(np.float64)


E2M1 = np.array([0.0, 0.5, 1.0, 1.5, 2.0, 3.0, 4.0, 6.0, -0.0, -0.5, -1.0, -1.5, -2.0, -3.0, -4.0, -6.0])


def pack_weight(w, fmt):
    k, n = w.shape
    w = f64(bf(w)).reshape(k // 32, 32, n)
    amax = np.abs(w).max(1)
    if fmt == "e4m3":
        byte = np.frexp(amax)[1] - 1 + 127 - 7
    else:
        mant, ex = np.frexp(amax / 6.0)
        byte = np.where(mant > 0.5, ex, ex - 1) + 127
    byte = np.clip(np.where(amax > 0, byte, 1), 1, 254)
    scaled = (w * np.exp2(127.0 - byte)[:, None, :]).reshape(k, n).astype(np.float32)
    by_word = np.ascontiguousarray(scaled.reshape(k // 512, 128, 4, n).transpose(0, 1, 3, 2))
    if fmt == "e4m3":
        words = by_word.astype(ml_dtypes.float8_e4m3fn).view(np.uint8)
    else:
        c = by_word.astype(ml_dtypes.float4_e2m1fn).view(np.uint8) & 0xF
        words = c[..., 0::2] | (c[..., 1::2] << 4)
    return np.ascontiguousarray(words), np.ascontiguousarray(byte.astype(np.uint8).reshape(k // 512, 16, n))


def unpack_weight(words, scales, fmt):
    g, p, n, _ = words.shape
    if fmt == "e4m3":
        vals = np.ascontiguousarray(words).view(ml_dtypes.float8_e4m3fn).astype(np.float64)
    else:
        nib = np.empty((g, p, n, 4), np.uint8)
        nib[..., 0::2] = words & 0xF
        nib[..., 1::2] = words >> 4
        vals = E2M1[nib]
    vals = vals * np.repeat(np.exp2(scales.astype(np.float64) - 127.0), 8, axis=1)[..., None]
    return vals.transpose(0, 1, 3, 2).reshape(g * 512, n)
def pack4(w):
    words, scales = pack_weight(w, "e2m1")
    return words.reshape(words.shape[0], 128, -1), scales


def unpack4(words, scales):
    return unpack_weight(words.reshape(words.shape[0], 128, -1, 2), scales, "e2m1")


M, K, N = 512, 1536, 2048

LOW, MID, HIGH = 0.6, 0.6, 0.7


def setup_inputs():
    s = mx_kscale(K)
    x = np.random.standard_normal((M, K)) * s
    low = LOW * np.random.standard_normal((K, N)) / np.sqrt(K) / s[:, None]
    mid = MID * np.random.standard_normal((K, N)) / np.sqrt(K) / s[:, None]
    high = HIGH * np.random.standard_normal((K, N)) / np.sqrt(K) / s[:, None]
    low_words, low_scales = pack4(low)
    mid_words, mid_scales = pack_weight(mid, "e4m3")
    return {"x": bf(x),
            "low_words": low_words, "low_scales": low_scales,
            "mid_words": mid_words, "mid_scales": mid_scales,
            "high": bf(high),
            "c": bf(1 + 0.1 * np.random.standard_normal(N))}


def reference(x, low_words, low_scales, mid_words, mid_scales, high, c):
    xq = mxq(f64(x), 1, "e4m3")
    y1 = xq @ unpack4(low_words, low_scales)
    y2 = xq @ unpack_weight(mid_words, mid_scales, "e4m3")
    y3 = xq @ mxq(f64(high), 0, "e4m3")
    y = y1 + y2 + y3 * f64(c)
    return y * y

@@ -1,0 +1,315 @@
+from contextlib import ExitStack
+
+import concourse.mybir as mybir
+from concourse.masks import make_identity
+
+M, K, N = 512, 1536, 2048
+FLOPS = 3 * 2 * M * K * N
+
+F32 = mybir.dt.float32
+BF16 = mybir.dt.bfloat16
+I32 = mybir.dt.int32
+U32 = mybir.dt.uint32
+U8 = mybir.dt.uint8
+FP8X4 = mybir.dt.float8_e4m3fn_x4
+FP4X4 = mybir.dt.float4_e2m1fn_x4
+ALU = mybir.AluOpType
+ACT = mybir.ActivationFunctionType
+
+P = 128
+PACK = 4
+K_PASS = P * PACK
+PASSES = K // K_PASS
+N_TILE = 512
+M_TILES = M // P
+N_TILES = N // N_TILE
+TILES = M_TILES * N_TILES
+PIECES = N_TILES * PASSES
+BANKS = 8
+MID_ROW = 4
+LEAD = M_TILES
+HEAD_SHARE = 256
+STEADY_SHARE = 176
+
+
+def tile_broadband_bartlett_power_s10_kernel(
+    tc, x, low_words, low_scales, mid_words, mid_scales, high, c, out
+):
+    nc = tc.nc
+
+    with ExitStack() as ctx:
+        keep = ctx.enter_context(tc.tile_pool(name="keep", bufs=1))
+        work = ctx.enter_context(tc.tile_pool(name="work", bufs=2))
+        psum = ctx.enter_context(tc.psum_pool(name="psum", bufs=1))
+        ctx.enter_context(tc.manual_schedule())
+
+        free_banks = list(range(BANKS))
+
+        def take_bank():
+            b = free_banks.pop(0)
+            return b, psum.tile([P, N_TILE], F32, name="bank%d" % b, tag="bank%d" % b)
+
+        def cols(n):
+            return slice(n * N_TILE, (n + 1) * N_TILE)
+
+        ident = keep.tile([P, P], F32)
+        make_identity(nc, ident[:])
+        low_sc_first = keep.tile([P, PASSES, N_TILE], U8, align_bytes=64)
+        low_sc_rest = keep.tile([P, PASSES, N - N_TILE], U8, align_bytes=64)
+        mid_sc = keep.tile([P, PASSES, N], U8, align_bytes=64)
+        for plane in (low_sc_first, mid_sc, low_sc_rest):
+            nc.vector.memset(plane[:].bitcast(I32), 0)
+
+        def load_scales(queue, plane, row0, scales, n0, n1):
+            for r in range(4):
+                queue.dma_start(
+                    out=plane[:].bitcast(I32)[row0 + r : P : 32],
+                    in_=scales[:, r:16:4, n0:n1].rearrange("g q n -> q g n").bitcast(I32),
+                )
+
+        x_raw, low, mid, high_raw = {}, {}, {}, {}
+
+        def load_x(m):
+            x_raw[m] = keep.tile([P, K], BF16, name="x_raw%d" % m)
+            nc.sync.dma_start(out=x_raw[m][:], in_=x[m * P : (m + 1) * P, :])
+
+        def load_low(n):
+            low[n] = keep.tile([P, PASSES, 2 * N_TILE], U8, name="low%d" % n, align_bytes=64)
+            src = low_words.rearrange("g p b -> p g b")[:, :, 2 * n * N_TILE : 2 * (n + 1) * N_TILE]
+            nc.sync.dma_start(out=low[n][:].bitcast(I32), in_=src.bitcast(I32))
+
+        def load_mid(n):
+            mid[n] = keep.tile([P, PASSES, N_TILE], U32, name="mid%d" % n, align_bytes=64)
+            src = mid_words.rearrange("g p n t -> p g (n t)")[:, :, 4 * n * N_TILE : 4 * (n + 1) * N_TILE]
+            nc.sync.dma_start(out=mid[n][:].bitcast(I32), in_=src.bitcast(I32))
+
+        def load_high(n):
+            for g in range(PASSES):
+                i = n * PASSES + g
+                high_raw[i] = keep.tile([P, PACK, N_TILE], BF16, name="high_raw%d" % i)
+                rows = high[g * K_PASS : (g + 1) * K_PASS, cols(n)]
+                nc.sync.dma_start(out=high_raw[i][:], in_=rows.rearrange("(p j) n -> p j n", j=PACK))
+
+        c_rows = keep.tile([P, N // P], BF16)
+        load_x(0)
+        load_low(0)
+        load_scales(nc.sync, low_sc_first, 0, low_scales, 0, N_TILE)
+        nc.sync.dma_start(out=c_rows[:], in_=c.rearrange("(p j) -> p j", p=P))
+        for m in range(1, M_TILES):
+            load_x(m)
+        load_mid(0)
+        load_high(0)
+        load_scales(nc.sync, low_sc_rest, 0, low_scales, N_TILE, N)
+        for n in range(1, N_TILES):
+            load_low(n)
+            load_mid(n)
+            load_high(n)
+        load_scales(nc.gpsimd, mid_sc, MID_ROW, mid_scales, 0, N)
+
+        x_sorted, x_grouped, x_codes, x_scales = {}, {}, {}, {}
+        X_PARTS = ((0, 1), (1, PASSES))
+
+        def sort_x(m):
+            x_sorted[m] = work.tile([P, 2, K // 4], F32, name="x_sorted", tag="x_sorted")
+            nc.vector.tensor_copy(
+                out=x_sorted[m][:], in_=x_raw[m][:].bitcast(F32).rearrange("r (w u) -> r u w", u=2)
+            )
+
+        def turn_x(m):
+            for part, (g0, g1) in enumerate(X_PARTS):
+                b, bank = take_bank()
+                for g in range(g0, g1):
+                    for u in range(2):
+                        if m == 0:
+                            src = x_raw[m][:].bitcast(F32)[:, 2 * P * g + u : 2 * P * (g + 1) : 2]
+                        else:
+                            src = x_sorted[m][:, u, P * g : P * (g + 1)]
+                        at = (2 * (g - g0) + u) * P
+                        nc.tensor.transpose(bank[:, at : at + P], src, ident[:])
+                width = (g1 - g0) * K_PASS
+                grouped = work.tile(
+                    [P, width], BF16, name="x_grouped%d" % part, tag="x_grouped%d" % part, align_bytes=64
+                )
+                nc.scalar.copy(
+                    out=grouped[:].bitcast(F32).rearrange("p (g r u) -> p g r u", r=P, u=2),
+                    in_=bank[:, : width // 2].rearrange("p (g u r) -> p g r u", r=P, u=2),
+                )
+                x_grouped[m, part] = grouped
+                free_banks.append(b)
+
+        def quantize_x(m, part):
+            if part == 0:
+                x_codes[m] = keep.tile([P, PASSES * P], U32, name="x_codes%d" % m, align_bytes=64)
+                x_scales[m] = keep.tile([P, PASSES * P], U8, name="x_scales%d" % m, align_bytes=64)
+            g0, g1 = X_PARTS[part]
+            nc.vector.quantize_mx(
+                out=x_codes[m][:, g0 * P : g1 * P].bitcast(FP8X4),
+                scales=x_scales[m][:, g0 * P : g1 * P],
+                in_=x_grouped[m, part][:],
+            )
+
+        c_all = keep.tile([P, N], BF16)
+
+        def spread_c():
+            words = c_rows[:].bitcast(F32)
+            for h in range(2):
+                b, bank = take_bank()
+                for w in range(4):
+                    col = words[:, 4 * h + w : 4 * h + w + 1].to_broadcast([P, P])
+                    nc.tensor.transpose(bank[:, w * P : (w + 1) * P], col, ident[:])
+                nc.scalar.copy(
+                    out=c_all[:].bitcast(F32).rearrange("q (p w) -> q p w", w=8)[:, :, 4 * h : 4 * h + 4],
+                    in_=bank[:].rearrange("q (w p) -> q p w", w=4),
+                )
+                free_banks.append(b)
+
+        high_grouped, high_codes, high_scales = {}, {}, {}
+
+        def interleave(engine_copy, i, n0, n1):
+            engine_copy(
+                out=high_grouped[i][:, n0:n1, :].rearrange("p (c i) t -> p c t i", i=4),
+                in_=high_raw[i][:, :, n0:n1].rearrange("p t (c i) -> p c t i", i=4),
+            )
+
+        def interleave_scalar(i, share):
+            high_grouped[i] = work.tile(
+                [P, N_TILE, PACK], BF16, name="high_grouped", tag="high_grouped", bufs=3, align_bytes=64
+            )
+            interleave(nc.scalar.copy, i, share, N_TILE)
+
+        def interleave_vector(i, share):
+            interleave(nc.vector.tensor_copy, i, 0, share)
+
+        def quantize_high(i):
+            high_codes[i] = keep.tile([P, N_TILE], U32, name="high_codes%d" % i, align_bytes=64)
+            high_scales[i] = keep.tile([P, N_TILE], U8, name="high_scales%d" % i, align_bytes=64)
+            nc.vector.quantize_mx(
+                out=high_codes[i][:].bitcast(FP8X4),
+                scales=high_scales[i][:],
+                in_=high_grouped[i][:].rearrange("p n t -> p (n t)"),
+            )
+
+        sum12, sum3, weighted = {}, {}, {}
+
+        def product(bank, j, codes, scales, first, last):
+            m = j % M_TILES
+            for g in range(PASSES):
+                nc.tensor.matmul_mx(
+                    out=bank[:],
+                    lhsT=x_codes[m][:, g * P : (g + 1) * P].bitcast(FP8X4),
+                    lhsT_scale=x_scales[m][:, g * P : (g + 1) * P],
+                    rhs=codes(g),
+                    rhs_scale=scales(g),
+                    start=first and g == 0,
+                    stop=last and g == PASSES - 1,
+                )
+
+        def low_product(j):
+            n = j // M_TILES
+            sum12[j] = take_bank()
+            plane, at = (low_sc_first, 0) if n == 0 else (low_sc_rest, n - 1)
+            product(
+                sum12[j][1], j, lambda g: low[n][:, g, :].bitcast(FP4X4), lambda g: plane[:, g, cols(at)], True, False
+            )
+
+        def mid_product(j):
+            n = j // M_TILES
+            product(
+                sum12[j][1],
+                j,
+                lambda g: mid[n][:, g, :].bitcast(FP8X4),
+                lambda g: mid_sc[MID_ROW:P, g, cols(n)],
+                False,
+                True,
+            )
+
+        def high_product(j):
+            i0 = j // M_TILES * PASSES
+            sum3[j] = take_bank()
+            product(
+                sum3[j][1],
+                j,
+                lambda g: high_codes[i0 + g][:].bitcast(FP8X4),
+                lambda g: high_scales[i0 + g][:],
+                True,
+                True,
+            )
+
+        def weigh(j):
+            b, bank = sum3[j]
+            weighted[j] = work.tile([P, N_TILE], F32, name="weighted", tag="weighted")
+            nc.vector.tensor_tensor(out=weighted[j][:], in0=bank[:], in1=c_all[:, cols(j // M_TILES)], op=ALU.mult)
+            free_banks.append(b)
+
+        def finish(j, parts=1):
+            b, bank = sum12[j]
+            m, n = j % M_TILES, j // M_TILES
+            width = N_TILE // parts
+            for s in range(parts):
+                part = slice(s * width, (s + 1) * width)
+                total = work.tile([P, width], F32, name="total", tag="total")
+                nc.vector.tensor_tensor(out=total[:], in0=bank[:, part], in1=weighted[j][:, part], op=ALU.add)
+                power = keep.tile([P, width], F32, name="power%d_%d" % (j, s))
+                nc.scalar.activation(out=power[:], in_=total[:], func=ACT.Square)
+                n0 = n * N_TILE + s * width
+                nc.sync.dma_start(out=out[m * P : (m + 1) * P, n0 : n0 + width], in_=power[:])
+            free_banks.append(b)
+
+        turn_x(0)
+        spread_c()
+        quantize_x(0, 0)
+        quantize_x(0, 1)
+        low_product(0)
+        sort_x(1)
+        turn_x(1)
+        sort_x(2)
+        turn_x(2)
+        quantize_x(1, 0)
+        sort_x(3)
+        quantize_x(1, 1)
+        low_product(1)
+        quantize_x(2, 0)
+        quantize_x(2, 1)
+        turn_x(3)
+        low_product(2)
+        mid_product(0)
+        quantize_x(3, 0)
+        quantize_x(3, 1)
+        low_product(3)
+        for j in range(1, LEAD):
+            mid_product(j)
+        for i in range(PASSES):
+            interleave_scalar(i, HEAD_SHARE)
+            interleave_vector(i, HEAD_SHARE)
+            if i > 0:
+                quantize_high(i - 1)
+        quantize_high(PASSES - 1)
+
+        steady = TILES - 2 * LEAD
+        for j in range(steady):
+            i = PASSES + j
+            low_product(j + LEAD)
+            high_product(j)
+            mid_product(j + LEAD)
+            interleave_scalar(i, STEADY_SHARE)
+            weigh(j)
+            interleave_vector(i, STEADY_SHARE)
+            finish(j)
+            quantize_high(i)
+
+        for s in range(LEAD):
+            j = steady + 2 * s
+            high_product(j)
+            high_product(j + 1)
+            low_product(steady + LEAD + s)
+            mid_product(steady + LEAD + s)
+            if s == 0:
+                interleave_scalar(PIECES - 1, STEADY_SHARE)
+            weigh(j)
+            if s == 0:
+                interleave_vector(PIECES - 1, STEADY_SHARE)
+            weigh(j + 1)
+            finish(j)
+            if s == 0:
+                quantize_high(PIECES - 1)
+            finish(j + 1, 2 if j + 1 == TILES - 1 else 1)

@@ -27,9 +27,9 @@ TILES = M_TILES * N_TILES
 PIECES = N_TILES * PASSES
 BANKS = 8
 MID_ROW = 4
-LEAD = M_TILES
 HEAD_SHARE = 256
-STEADY_SHARE = 176
+STEADY_SHARE = 136
+HALF = N // 2
 
 
 def tile_broadband_bartlett_power_s10_kernel(
@@ -56,8 +56,9 @@ def tile_broadband_bartlett_power_s10_kernel(
         make_identity(nc, ident[:])
         low_sc_first = keep.tile([P, PASSES, N_TILE], U8, align_bytes=64)
         low_sc_rest = keep.tile([P, PASSES, N - N_TILE], U8, align_bytes=64)
-        mid_sc = keep.tile([P, PASSES, N], U8, align_bytes=64)
-        for plane in (low_sc_first, mid_sc, low_sc_rest):
+        mid_sc_first = keep.tile([P, PASSES, HALF], U8, align_bytes=64)
+        mid_sc_second = keep.tile([P, PASSES, HALF], U8, align_bytes=64)
+        for plane in (low_sc_first, low_sc_rest, mid_sc_first, mid_sc_second):
             nc.vector.memset(plane[:].bitcast(I32), 0)
 
         def load_scales(queue, plane, row0, scales, n0, n1):
@@ -91,26 +92,28 @@ def tile_broadband_bartlett_power_s10_kernel(
                 nc.sync.dma_start(out=high_raw[i][:], in_=rows.rearrange("(p j) n -> p j n", j=PACK))
 
         c_rows = keep.tile([P, N // P], BF16)
+        nc.sync.dma_start(out=c_rows[:], in_=c.rearrange("(p j) -> p j", p=P))
         load_x(0)
+        load_x(1)
+        load_x(2)
         load_low(0)
         load_scales(nc.sync, low_sc_first, 0, low_scales, 0, N_TILE)
-        nc.sync.dma_start(out=c_rows[:], in_=c.rearrange("(p j) -> p j", p=P))
-        for m in range(1, M_TILES):
-            load_x(m)
+        load_x(3)
         load_mid(0)
+        load_scales(nc.sync, mid_sc_first, MID_ROW, mid_scales, 0, HALF)
         load_high(0)
-        load_scales(nc.sync, low_sc_rest, 0, low_scales, N_TILE, N)
         for n in range(1, N_TILES):
             load_low(n)
             load_mid(n)
             load_high(n)
-        load_scales(nc.gpsimd, mid_sc, MID_ROW, mid_scales, 0, N)
+        load_scales(nc.gpsimd, low_sc_rest, 0, low_scales, N_TILE, N)
+        load_scales(nc.gpsimd, mid_sc_second, MID_ROW, mid_scales, HALF, N)
 
         x_sorted, x_grouped, x_codes, x_scales = {}, {}, {}, {}
         X_PARTS = ((0, 1), (1, PASSES))
 
         def sort_x(m):
-            x_sorted[m] = work.tile([P, 2, K // 4], F32, name="x_sorted", tag="x_sorted")
+            x_sorted[m] = work.tile([P, 2, K // 4], F32, name="x_sorted", tag="x_sorted", bufs=3)
             nc.vector.tensor_copy(
                 out=x_sorted[m][:], in_=x_raw[m][:].bitcast(F32).rearrange("r (w u) -> r u w", u=2)
             )
@@ -120,10 +123,7 @@ def tile_broadband_bartlett_power_s10_kernel(
                 b, bank = take_bank()
                 for g in range(g0, g1):
                     for u in range(2):
-                        if m == 0:
-                            src = x_raw[m][:].bitcast(F32)[:, 2 * P * g + u : 2 * P * (g + 1) : 2]
-                        else:
-                            src = x_sorted[m][:, u, P * g : P * (g + 1)]
+                        src = x_sorted[m][:, u, P * g : P * (g + 1)]
                         at = (2 * (g - g0) + u) * P
                         nc.tensor.transpose(bank[:, at : at + P], src, ident[:])
                 width = (g1 - g0) * K_PASS
@@ -137,26 +137,30 @@ def tile_broadband_bartlett_power_s10_kernel(
                 x_grouped[m, part] = grouped
                 free_banks.append(b)
 
-        def quantize_x(m, part):
-            if part == 0:
-                x_codes[m] = keep.tile([P, PASSES * P], U32, name="x_codes%d" % m, align_bytes=64)
-                x_scales[m] = keep.tile([P, PASSES * P], U8, name="x_scales%d" % m, align_bytes=64)
-            g0, g1 = X_PARTS[part]
-            nc.vector.quantize_mx(
-                out=x_codes[m][:, g0 * P : g1 * P].bitcast(FP8X4),
-                scales=x_scales[m][:, g0 * P : g1 * P],
-                in_=x_grouped[m, part][:],
-            )
+        def quantize_x(m):
+            for part, (g0, g1) in enumerate(X_PARTS):
+                width = (g1 - g0) * P
+                codes = keep.tile([P, width], U32, name="x_codes%d_%d" % (m, part), align_bytes=64)
+                scales = keep.tile([P, width], U8, name="x_scales%d_%d" % (m, part), align_bytes=64)
+                nc.vector.quantize_mx(out=codes[:].bitcast(FP8X4), scales=scales[:], in_=x_grouped[m, part][:])
+                for g in range(g0, g1):
+                    x_codes[m, g] = codes[:, (g - g0) * P : (g - g0 + 1) * P]
+                    x_scales[m, g] = scales[:, (g - g0) * P : (g - g0 + 1) * P]
 
         c_all = keep.tile([P, N], BF16)
 
-        def spread_c():
+        c_banks = []
+
+        def turn_c():
             words = c_rows[:].bitcast(F32)
             for h in range(2):
-                b, bank = take_bank()
+                c_banks.append(take_bank())
                 for w in range(4):
                     col = words[:, 4 * h + w : 4 * h + w + 1].to_broadcast([P, P])
-                    nc.tensor.transpose(bank[:, w * P : (w + 1) * P], col, ident[:])
+                    nc.tensor.transpose(c_banks[h][1][:, w * P : (w + 1) * P], col, ident[:])
+
+        def copy_c():
+            for h, (b, bank) in enumerate(c_banks):
                 nc.scalar.copy(
                     out=c_all[:].bitcast(F32).rearrange("q (p w) -> q p w", w=8)[:, :, 4 * h : 4 * h + 4],
                     in_=bank[:].rearrange("q (w p) -> q p w", w=4),
@@ -189,15 +193,15 @@ def tile_broadband_bartlett_power_s10_kernel(
                 in_=high_grouped[i][:].rearrange("p n t -> p (n t)"),
             )
 
-        sum12, sum3, weighted = {}, {}, {}
+        sum12, sum3, weighted, total = {}, {}, {}, {}
 
         def product(bank, j, codes, scales, first, last):
             m = j % M_TILES
             for g in range(PASSES):
                 nc.tensor.matmul_mx(
                     out=bank[:],
-                    lhsT=x_codes[m][:, g * P : (g + 1) * P].bitcast(FP8X4),
-                    lhsT_scale=x_scales[m][:, g * P : (g + 1) * P],
+                    lhsT=x_codes[m, g].bitcast(FP8X4),
+                    lhsT_scale=x_scales[m, g],
                     rhs=codes(g),
                     rhs_scale=scales(g),
                     start=first and g == 0,
@@ -214,11 +218,12 @@ def tile_broadband_bartlett_power_s10_kernel(
 
         def mid_product(j):
             n = j // M_TILES
+            plane = mid_sc_first if n < 2 else mid_sc_second
             product(
                 sum12[j][1],
                 j,
                 lambda g: mid[n][:, g, :].bitcast(FP8X4),
-                lambda g: mid_sc[MID_ROW:P, g, cols(n)],
+                lambda g: plane[MID_ROW:P, g, cols(n % 2)],
                 False,
                 True,
             )
@@ -241,75 +246,82 @@ def tile_broadband_bartlett_power_s10_kernel(
             nc.vector.tensor_tensor(out=weighted[j][:], in0=bank[:], in1=c_all[:, cols(j // M_TILES)], op=ALU.mult)
             free_banks.append(b)
 
-        def finish(j, parts=1):
+        def add_up(j, parts):
             b, bank = sum12[j]
-            m, n = j % M_TILES, j // M_TILES
             width = N_TILE // parts
             for s in range(parts):
                 part = slice(s * width, (s + 1) * width)
-                total = work.tile([P, width], F32, name="total", tag="total")
-                nc.vector.tensor_tensor(out=total[:], in0=bank[:, part], in1=weighted[j][:, part], op=ALU.add)
-                power = keep.tile([P, width], F32, name="power%d_%d" % (j, s))
-                nc.scalar.activation(out=power[:], in_=total[:], func=ACT.Square)
-                n0 = n * N_TILE + s * width
-                nc.sync.dma_start(out=out[m * P : (m + 1) * P, n0 : n0 + width], in_=power[:])
+                total[j, s] = work.tile([P, width], F32, name="total", tag="total", bufs=6)
+                nc.vector.tensor_tensor(out=total[j, s][:], in0=bank[:, part], in1=weighted[j][:, part], op=ALU.add)
             free_banks.append(b)
 
-        turn_x(0)
-        spread_c()
-        quantize_x(0, 0)
-        quantize_x(0, 1)
-        low_product(0)
+        def square_and_store(j, parts):
+            m, n = j % M_TILES, j // M_TILES
+            width = N_TILE // parts
+            for s in range(parts):
+                power = keep.tile([P, width], F32, name="power%d_%d" % (j, s))
+                nc.scalar.activation(out=power[:], in_=total[j, s][:], func=ACT.Square)
+                n0 = n * N_TILE + s * width
+                nc.sync.dma_start(out=out[m * P : (m + 1) * P, n0 : n0 + width], in_=power[:])
+
+        turn_c()
+        copy_c()
+        sort_x(0)
         sort_x(1)
-        turn_x(1)
         sort_x(2)
+        turn_x(0)
+        turn_x(1)
+        quantize_x(0)
+        quantize_x(1)
         turn_x(2)
-        quantize_x(1, 0)
-        sort_x(3)
-        quantize_x(1, 1)
+        quantize_x(2)
+        low_product(0)
         low_product(1)
-        quantize_x(2, 0)
-        quantize_x(2, 1)
-        turn_x(3)
         low_product(2)
+        sort_x(3)
+        turn_x(3)
+        quantize_x(3)
         mid_product(0)
-        quantize_x(3, 0)
-        quantize_x(3, 1)
+        mid_product(1)
+        mid_product(2)
         low_product(3)
-        for j in range(1, LEAD):
-            mid_product(j)
+        mid_product(3)
         for i in range(PASSES):
             interleave_scalar(i, HEAD_SHARE)
             interleave_vector(i, HEAD_SHARE)
             if i > 0:
                 quantize_high(i - 1)
         quantize_high(PASSES - 1)
+        low_product(M_TILES)
+        low_product(M_TILES + 1)
 
-        steady = TILES - 2 * LEAD
-        for j in range(steady):
-            i = PASSES + j
-            low_product(j + LEAD)
-            high_product(j)
-            mid_product(j + LEAD)
-            interleave_scalar(i, STEADY_SHARE)
-            weigh(j)
-            interleave_vector(i, STEADY_SHARE)
-            finish(j)
-            quantize_high(i)
+        ahead = []
+        for j in range(M_TILES, TILES):
+            ahead.append((mid_product, j))
+            if j + 2 < TILES:
+                ahead.append((low_product, j + 2))
 
-        for s in range(LEAD):
-            j = steady + 2 * s
+        def run_ahead(count):
+            for s in range(count):
+                half, j = ahead.pop(0)
+                half(j)
+
+        piece_steps = [0,1,2,4,5,6,8,9,10]
+        counts = [2,2,1,1,2,2,1,1,2,2,1,1,1,1,1,1]
+        for j in range(TILES):
+            piece = j in piece_steps
+            i = PASSES + piece_steps.index(j) if piece else 0
             high_product(j)
-            high_product(j + 1)
-            low_product(steady + LEAD + s)
-            mid_product(steady + LEAD + s)
-            if s == 0:
-                interleave_scalar(PIECES - 1, STEADY_SHARE)
+            run_ahead(counts[j])
+            if piece:
+                interleave_scalar(i, STEADY_SHARE)
             weigh(j)
-            if s == 0:
-                interleave_vector(PIECES - 1, STEADY_SHARE)
-            weigh(j + 1)
-            finish(j)
-            if s == 0:
-                quantize_high(PIECES - 1)
-            finish(j + 1, 2 if j + 1 == TILES - 1 else 1)
+            if piece and STEADY_SHARE:
+                interleave_vector(i, STEADY_SHARE)
+            add_up(j, 2 if j == TILES - 1 else 1)
+            if j >= 4:
+                square_and_store(j - 4, 1)
+            if piece:
+                quantize_high(i)
+        for j in range(TILES - 4, TILES):
+            square_and_store(j, 2 if j == TILES - 1 else 1)

@@ -28,7 +28,7 @@ PIECES = N_TILES * PASSES
 BANKS = 8
 MID_ROW = 4
 HEAD_SHARE = 256
-STEADY_SHARE = 136
+STEADY_SHARE = 144
 HALF = N // 2
 
 
@@ -54,19 +54,19 @@ def tile_broadband_bartlett_power_s10_kernel(
 
         ident = keep.tile([P, P], F32)
         make_identity(nc, ident[:])
-        low_sc_first = keep.tile([P, PASSES, N_TILE], U8, align_bytes=64)
-        low_sc_rest = keep.tile([P, PASSES, N - N_TILE], U8, align_bytes=64)
+        low_sc_first = keep.tile([P, PASSES, HALF], U8, align_bytes=64)
         mid_sc_first = keep.tile([P, PASSES, HALF], U8, align_bytes=64)
-        mid_sc_second = keep.tile([P, PASSES, HALF], U8, align_bytes=64)
-        for plane in (low_sc_first, low_sc_rest, mid_sc_first, mid_sc_second):
+        sc_second = keep.tile([P, PASSES, HALF], U8, align_bytes=64)
+        for plane in (low_sc_first, mid_sc_first, sc_second):
             nc.vector.memset(plane[:].bitcast(I32), 0)
 
-        def load_scales(queue, plane, row0, scales, n0, n1):
+        def load_scales(plane, sources, n0, n1):
             for r in range(4):
-                queue.dma_start(
-                    out=plane[:].bitcast(I32)[row0 + r : P : 32],
-                    in_=scales[:, r:16:4, n0:n1].rearrange("g q n -> q g n").bitcast(I32),
-                )
+                for row0, scales in sources:
+                    nc.sync.dma_start(
+                        out=plane[:].bitcast(I32)[row0 + r : P : 32],
+                        in_=scales[:, r:16:4, n0:n1].rearrange("g q n -> q g n").bitcast(I32),
+                    )
 
         x_raw, low, mid, high_raw = {}, {}, {}, {}
 
@@ -84,30 +84,32 @@ def tile_broadband_bartlett_power_s10_kernel(
             src = mid_words.rearrange("g p n t -> p g (n t)")[:, :, 4 * n * N_TILE : 4 * (n + 1) * N_TILE]
             nc.sync.dma_start(out=mid[n][:].bitcast(I32), in_=src.bitcast(I32))
 
-        def load_high(n):
-            for g in range(PASSES):
-                i = n * PASSES + g
-                high_raw[i] = keep.tile([P, PACK, N_TILE], BF16, name="high_raw%d" % i)
-                rows = high[g * K_PASS : (g + 1) * K_PASS, cols(n)]
-                nc.sync.dma_start(out=high_raw[i][:], in_=rows.rearrange("(p j) n -> p j n", j=PACK))
+        def load_high(n, g):
+            i = n * PASSES + g
+            high_raw[i] = keep.tile([P, PACK, N_TILE], BF16, name="high_raw%d" % i)
+            rows = high[g * K_PASS : (g + 1) * K_PASS, cols(n)]
+            nc.sync.dma_start(out=high_raw[i][:], in_=rows.rearrange("(p j) n -> p j n", j=PACK))
 
         c_rows = keep.tile([P, N // P], BF16)
         nc.sync.dma_start(out=c_rows[:], in_=c.rearrange("(p j) -> p j", p=P))
-        load_x(0)
-        load_x(1)
-        load_x(2)
+        for m in range(M_TILES - 1):
+            load_x(m)
         load_low(0)
-        load_scales(nc.sync, low_sc_first, 0, low_scales, 0, N_TILE)
-        load_x(3)
+        load_scales(low_sc_first, [(0, low_scales)], 0, HALF)
+        load_x(M_TILES - 1)
         load_mid(0)
-        load_scales(nc.sync, mid_sc_first, MID_ROW, mid_scales, 0, HALF)
-        load_high(0)
+        load_scales(mid_sc_first, [(MID_ROW, mid_scales)], 0, HALF)
+        for g in range(PASSES):
+            load_high(0, g)
         for n in range(1, N_TILES):
             load_low(n)
+            if n == N_TILES // 2:
+                load_scales(sc_second, [(0, low_scales), (MID_ROW, mid_scales)], HALF, N)
+            for g in range(1):
+                load_high(n, g)
             load_mid(n)
-            load_high(n)
-        load_scales(nc.gpsimd, low_sc_rest, 0, low_scales, N_TILE, N)
-        load_scales(nc.gpsimd, mid_sc_second, MID_ROW, mid_scales, HALF, N)
+            for g in range(1, PASSES):
+                load_high(n, g)
 
         x_sorted, x_grouped, x_codes, x_scales = {}, {}, {}, {}
         X_PARTS = ((0, 1), (1, PASSES))
@@ -170,10 +172,7 @@ def tile_broadband_bartlett_power_s10_kernel(
         high_grouped, high_codes, high_scales = {}, {}, {}
 
         def interleave(engine_copy, i, n0, n1):
-            engine_copy(
-                out=high_grouped[i][:, n0:n1, :].rearrange("p (c i) t -> p c t i", i=4),
-                in_=high_raw[i][:, :, n0:n1].rearrange("p t (c i) -> p c t i", i=4),
-            )
+            engine_copy(out=high_grouped[i][:, n0:n1, :], in_=high_raw[i][:, :, n0:n1].rearrange("p t n -> p n t"))
 
         def interleave_scalar(i, share):
             high_grouped[i] = work.tile(
@@ -211,14 +210,14 @@ def tile_broadband_bartlett_power_s10_kernel(
         def low_product(j):
             n = j // M_TILES
             sum12[j] = take_bank()
-            plane, at = (low_sc_first, 0) if n == 0 else (low_sc_rest, n - 1)
+            plane, at = (low_sc_first, n) if n < 2 else (sc_second, n - 2)
             product(
                 sum12[j][1], j, lambda g: low[n][:, g, :].bitcast(FP4X4), lambda g: plane[:, g, cols(at)], True, False
             )
 
         def mid_product(j):
             n = j // M_TILES
-            plane = mid_sc_first if n < 2 else mid_sc_second
+            plane = mid_sc_first if n < 2 else sc_second
             product(
                 sum12[j][1],
                 j,
@@ -251,7 +250,7 @@ def tile_broadband_bartlett_power_s10_kernel(
             width = N_TILE // parts
             for s in range(parts):
                 part = slice(s * width, (s + 1) * width)
-                total[j, s] = work.tile([P, width], F32, name="total", tag="total", bufs=6)
+                total[j, s] = work.tile([P, width], F32, name="total", tag="total", bufs=4)
                 nc.vector.tensor_tensor(out=total[j, s][:], in0=bank[:, part], in1=weighted[j][:, part], op=ALU.add)
             free_banks.append(b)
 
@@ -319,9 +318,9 @@ def tile_broadband_bartlett_power_s10_kernel(
             if piece and STEADY_SHARE:
                 interleave_vector(i, STEADY_SHARE)
             add_up(j, 2 if j == TILES - 1 else 1)
-            if j >= 4:
-                square_and_store(j - 4, 1)
+            if j >= 2:
+                square_and_store(j - 2, 1)
             if piece:
                 quantize_high(i)
-        for j in range(TILES - 4, TILES):
+        for j in range(TILES - 2, TILES):
             square_and_store(j, 2 if j == TILES - 1 else 1)

@@ -24,12 +24,16 @@ N_TILE = 512
 M_TILES = M // P
 N_TILES = N // N_TILE
 TILES = M_TILES * N_TILES
-PIECES = N_TILES * PASSES
 BANKS = 8
+QUADRANT = 32
+SCALE_ROWS = 4
+BLOCKS = K_PASS // 32
 MID_ROW = 4
+C_WORDS = N // P // 2
+X_PARTS = ((0, 1), (1, PASSES))
 HEAD_SHARE = 256
 STEADY_SHARE = 144
-HALF = N // 2
+SQUARE_LAG = 2
 
 
 def tile_broadband_bartlett_power_s10_kernel(
@@ -54,18 +58,19 @@ def tile_broadband_bartlett_power_s10_kernel(
 
         ident = keep.tile([P, P], F32)
         make_identity(nc, ident[:])
-        low_sc_first = keep.tile([P, PASSES, HALF], U8, align_bytes=64)
-        mid_sc_first = keep.tile([P, PASSES, HALF], U8, align_bytes=64)
-        sc_second = keep.tile([P, PASSES, HALF], U8, align_bytes=64)
-        for plane in (low_sc_first, mid_sc_first, sc_second):
+
+        low_plane_first = keep.tile([P, PASSES, N_TILE], U8, align_bytes=64)
+        low_plane_rest = keep.tile([P, PASSES, N - N_TILE], U8, align_bytes=64)
+        mid_plane = keep.tile([P, PASSES, N], U8, align_bytes=64)
+        for plane in (low_plane_first, low_plane_rest, mid_plane):
             nc.vector.memset(plane[:].bitcast(I32), 0)
 
-        def load_scales(plane, sources, n0, n1):
-            for r in range(4):
-                for row0, scales in sources:
+        def load_scales(sources):
+            for r in range(SCALE_ROWS):
+                for plane, first_row, scales in sources:
                     nc.sync.dma_start(
-                        out=plane[:].bitcast(I32)[row0 + r : P : 32],
-                        in_=scales[:, r:16:4, n0:n1].rearrange("g q n -> q g n").bitcast(I32),
+                        out=plane[:].bitcast(I32)[first_row + r : P : QUADRANT],
+                        in_=scales[:, r:BLOCKS:SCALE_ROWS, :].rearrange("g q n -> q g n").bitcast(I32),
                     )
 
         x_raw, low, mid, high_raw = {}, {}, {}, {}
@@ -76,46 +81,44 @@ def tile_broadband_bartlett_power_s10_kernel(
 
         def load_low(n):
             low[n] = keep.tile([P, PASSES, 2 * N_TILE], U8, name="low%d" % n, align_bytes=64)
-            src = low_words.rearrange("g p b -> p g b")[:, :, 2 * n * N_TILE : 2 * (n + 1) * N_TILE]
-            nc.sync.dma_start(out=low[n][:].bitcast(I32), in_=src.bitcast(I32))
+            words = low_words.rearrange("g p b -> p g b")[:, :, 2 * n * N_TILE : 2 * (n + 1) * N_TILE]
+            nc.sync.dma_start(out=low[n][:].bitcast(I32), in_=words.bitcast(I32))
 
         def load_mid(n):
             mid[n] = keep.tile([P, PASSES, N_TILE], U32, name="mid%d" % n, align_bytes=64)
-            src = mid_words.rearrange("g p n t -> p g (n t)")[:, :, 4 * n * N_TILE : 4 * (n + 1) * N_TILE]
-            nc.sync.dma_start(out=mid[n][:].bitcast(I32), in_=src.bitcast(I32))
+            words = mid_words.rearrange("g p n t -> p g (n t)")[:, :, PACK * n * N_TILE : PACK * (n + 1) * N_TILE]
+            nc.sync.dma_start(out=mid[n][:].bitcast(I32), in_=words.bitcast(I32))
 
-        def load_high(n, g):
-            i = n * PASSES + g
-            high_raw[i] = keep.tile([P, PACK, N_TILE], BF16, name="high_raw%d" % i)
-            rows = high[g * K_PASS : (g + 1) * K_PASS, cols(n)]
-            nc.sync.dma_start(out=high_raw[i][:], in_=rows.rearrange("(p j) n -> p j n", j=PACK))
+        def load_high(n, passes):
+            for g in passes:
+                piece = n * PASSES + g
+                high_raw[piece] = keep.tile([P, PACK, N_TILE], BF16, name="high_raw%d" % piece)
+                rows = high[g * K_PASS : (g + 1) * K_PASS, cols(n)]
+                nc.sync.dma_start(out=high_raw[piece][:], in_=rows.rearrange("(p t) n -> p t n", t=PACK))
 
         c_rows = keep.tile([P, N // P], BF16)
-        nc.sync.dma_start(out=c_rows[:], in_=c.rearrange("(p j) -> p j", p=P))
-        for m in range(M_TILES - 1):
+        nc.sync.dma_start(out=c_rows[:], in_=c.rearrange("(p i) -> p i", p=P))
+        for m in range(M_TILES):
             load_x(m)
         load_low(0)
-        load_scales(low_sc_first, [(0, low_scales)], 0, HALF)
-        load_x(M_TILES - 1)
+        load_scales([(low_plane_first, 0, low_scales[:, :, :N_TILE])])
+        load_scales([(mid_plane, MID_ROW, mid_scales), (low_plane_rest, 0, low_scales[:, :, N_TILE:])])
         load_mid(0)
-        load_scales(mid_sc_first, [(MID_ROW, mid_scales)], 0, HALF)
-        for g in range(PASSES):
-            load_high(0, g)
-        for n in range(1, N_TILES):
+        load_high(0, range(PASSES - 1))
+        load_low(1)
+        load_high(0, [PASSES - 1])
+        load_mid(1)
+        load_high(1, range(PASSES))
+        for n in range(2, N_TILES):
             load_low(n)
-            if n == N_TILES // 2:
-                load_scales(sc_second, [(0, low_scales), (MID_ROW, mid_scales)], HALF, N)
-            for g in range(1):
-                load_high(n, g)
+            load_high(n, [0])
             load_mid(n)
-            for g in range(1, PASSES):
-                load_high(n, g)
+            load_high(n, range(1, PASSES))
 
         x_sorted, x_grouped, x_codes, x_scales = {}, {}, {}, {}
-        X_PARTS = ((0, 1), (1, PASSES))
 
         def sort_x(m):
-            x_sorted[m] = work.tile([P, 2, K // 4], F32, name="x_sorted", tag="x_sorted", bufs=3)
+            x_sorted[m] = work.tile([P, 2, K // PACK], F32, name="x_sorted", tag="x_sorted", bufs=3)
             nc.vector.tensor_copy(
                 out=x_sorted[m][:], in_=x_raw[m][:].bitcast(F32).rearrange("r (w u) -> r u w", u=2)
             )
@@ -125,9 +128,8 @@ def tile_broadband_bartlett_power_s10_kernel(
                 b, bank = take_bank()
                 for g in range(g0, g1):
                     for u in range(2):
-                        src = x_sorted[m][:, u, P * g : P * (g + 1)]
                         at = (2 * (g - g0) + u) * P
-                        nc.tensor.transpose(bank[:, at : at + P], src, ident[:])
+                        nc.tensor.transpose(bank[:, at : at + P], x_sorted[m][:, u, P * g : P * (g + 1)], ident[:])
                 width = (g1 - g0) * K_PASS
                 grouped = work.tile(
                     [P, width], BF16, name="x_grouped%d" % part, tag="x_grouped%d" % part, align_bytes=64
@@ -151,176 +153,165 @@ def tile_broadband_bartlett_power_s10_kernel(
 
         c_all = keep.tile([P, N], BF16)
 
-        c_banks = []
-
-        def turn_c():
+        def spread_c():
             words = c_rows[:].bitcast(F32)
-            for h in range(2):
-                c_banks.append(take_bank())
-                for w in range(4):
-                    col = words[:, 4 * h + w : 4 * h + w + 1].to_broadcast([P, P])
-                    nc.tensor.transpose(c_banks[h][1][:, w * P : (w + 1) * P], col, ident[:])
-
-        def copy_c():
-            for h, (b, bank) in enumerate(c_banks):
+            per_bank = N_TILE // P
+            taken = []
+            for w0 in range(0, C_WORDS, per_bank):
+                b, bank = take_bank()
+                taken.append((w0, b, bank))
+                for w in range(per_bank):
+                    repeated = words[:, w0 + w : w0 + w + 1].to_broadcast([P, P])
+                    nc.tensor.transpose(bank[:, w * P : (w + 1) * P], repeated, ident[:])
+            for w0, b, bank in taken:
                 nc.scalar.copy(
-                    out=c_all[:].bitcast(F32).rearrange("q (p w) -> q p w", w=8)[:, :, 4 * h : 4 * h + 4],
-                    in_=bank[:].rearrange("q (w p) -> q p w", w=4),
+                    out=c_all[:].bitcast(F32).rearrange("q (p w) -> q p w", w=C_WORDS)[:, :, w0 : w0 + per_bank],
+                    in_=bank[:].rearrange("q (w p) -> q p w", w=per_bank),
                 )
                 free_banks.append(b)
 
         high_grouped, high_codes, high_scales = {}, {}, {}
 
-        def interleave(engine_copy, i, n0, n1):
-            engine_copy(out=high_grouped[i][:, n0:n1, :], in_=high_raw[i][:, :, n0:n1].rearrange("p t n -> p n t"))
-
-        def interleave_scalar(i, share):
-            high_grouped[i] = work.tile(
-                [P, N_TILE, PACK], BF16, name="high_grouped", tag="high_grouped", bufs=3, align_bytes=64
+        def interleave(copy, piece, n0, n1):
+            copy(
+                out=high_grouped[piece][:, n0:n1, :],
+                in_=high_raw[piece][:, :, n0:n1].rearrange("p t n -> p n t"),
             )
-            interleave(nc.scalar.copy, i, share, N_TILE)
 
-        def interleave_vector(i, share):
-            interleave(nc.vector.tensor_copy, i, 0, share)
+        def interleave_scalar(piece, share):
+            high_grouped[piece] = work.tile(
+                [P, N_TILE, PACK], BF16, name="high_grouped", tag="high_grouped", bufs=PASSES, align_bytes=64
+            )
+            interleave(nc.scalar.copy, piece, share, N_TILE)
 
-        def quantize_high(i):
-            high_codes[i] = keep.tile([P, N_TILE], U32, name="high_codes%d" % i, align_bytes=64)
-            high_scales[i] = keep.tile([P, N_TILE], U8, name="high_scales%d" % i, align_bytes=64)
+        def interleave_vector(piece, share):
+            interleave(nc.vector.tensor_copy, piece, 0, share)
+
+        def quantize_high(piece):
+            high_codes[piece] = keep.tile([P, N_TILE], U32, name="high_codes%d" % piece, align_bytes=64)
+            high_scales[piece] = keep.tile([P, N_TILE], U8, name="high_scales%d" % piece, align_bytes=64)
             nc.vector.quantize_mx(
-                out=high_codes[i][:].bitcast(FP8X4),
-                scales=high_scales[i][:],
-                in_=high_grouped[i][:].rearrange("p n t -> p (n t)"),
+                out=high_codes[piece][:].bitcast(FP8X4),
+                scales=high_scales[piece][:],
+                in_=high_grouped[piece][:].rearrange("p n t -> p (n t)"),
             )
 
-        sum12, sum3, weighted, total = {}, {}, {}, {}
+        low_mid_bank, high_bank, weighted, total = {}, {}, {}, {}
+        whole = slice(0, N_TILE)
 
-        def product(bank, j, codes, scales, first, last):
+        def product(bank, j, window, codes, scales, opens, closes):
             m = j % M_TILES
             for g in range(PASSES):
                 nc.tensor.matmul_mx(
-                    out=bank[:],
+                    out=bank[:, window],
                     lhsT=x_codes[m, g].bitcast(FP8X4),
                     lhsT_scale=x_scales[m, g],
-                    rhs=codes(g),
-                    rhs_scale=scales(g),
-                    start=first and g == 0,
-                    stop=last and g == PASSES - 1,
+                    rhs=codes[g][:, window],
+                    rhs_scale=scales[g][:, window],
+                    start=opens and g == 0,
+                    stop=closes and g == PASSES - 1,
                 )
 
-        def low_product(j):
+        def low_product(j, window=whole):
             n = j // M_TILES
-            sum12[j] = take_bank()
-            plane, at = (low_sc_first, n) if n < 2 else (sc_second, n - 2)
-            product(
-                sum12[j][1], j, lambda g: low[n][:, g, :].bitcast(FP4X4), lambda g: plane[:, g, cols(at)], True, False
-            )
+            low_mid_bank[j] = take_bank()
+            plane, plane_cols = (low_plane_first, whole) if n == 0 else (low_plane_rest, cols(n - 1))
+            codes = [low[n][:, g, :].bitcast(FP4X4) for g in range(PASSES)]
+            scales = [plane[:, g, plane_cols] for g in range(PASSES)]
+            product(low_mid_bank[j][1], j, window, codes, scales, True, False)
 
-        def mid_product(j):
+        def mid_product(j, window=whole):
             n = j // M_TILES
-            plane = mid_sc_first if n < 2 else sc_second
-            product(
-                sum12[j][1],
-                j,
-                lambda g: mid[n][:, g, :].bitcast(FP8X4),
-                lambda g: plane[MID_ROW:P, g, cols(n % 2)],
-                False,
-                True,
-            )
+            codes = [mid[n][:, g, :].bitcast(FP8X4) for g in range(PASSES)]
+            scales = [mid_plane[MID_ROW:P, g, cols(n)] for g in range(PASSES)]
+            product(low_mid_bank[j][1], j, window, codes, scales, False, True)
 
         def high_product(j):
-            i0 = j // M_TILES * PASSES
-            sum3[j] = take_bank()
-            product(
-                sum3[j][1],
-                j,
-                lambda g: high_codes[i0 + g][:].bitcast(FP8X4),
-                lambda g: high_scales[i0 + g][:],
-                True,
-                True,
-            )
+            pieces = range(j // M_TILES * PASSES, (j // M_TILES + 1) * PASSES)
+            high_bank[j] = take_bank()
+            codes = [high_codes[piece][:].bitcast(FP8X4) for piece in pieces]
+            scales = [high_scales[piece][:] for piece in pieces]
+            product(high_bank[j][1], j, whole, codes, scales, True, True)
 
         def weigh(j):
-            b, bank = sum3[j]
+            b, bank = high_bank[j]
             weighted[j] = work.tile([P, N_TILE], F32, name="weighted", tag="weighted")
             nc.vector.tensor_tensor(out=weighted[j][:], in0=bank[:], in1=c_all[:, cols(j // M_TILES)], op=ALU.mult)
             free_banks.append(b)
 
-        def add_up(j, parts):
-            b, bank = sum12[j]
-            width = N_TILE // parts
-            for s in range(parts):
-                part = slice(s * width, (s + 1) * width)
-                total[j, s] = work.tile([P, width], F32, name="total", tag="total", bufs=4)
-                nc.vector.tensor_tensor(out=total[j, s][:], in0=bank[:, part], in1=weighted[j][:, part], op=ALU.add)
+        def add_up(j, window=whole):
+            b, bank = low_mid_bank[j]
+            total[j] = work.tile(
+                [P, window.stop - window.start], F32, name="total", tag="total", bufs=SQUARE_LAG + 2
+            )
+            nc.vector.tensor_tensor(out=total[j][:], in0=bank[:, window], in1=weighted[j][:, window], op=ALU.add)
             free_banks.append(b)
 
-        def square_and_store(j, parts):
-            m, n = j % M_TILES, j // M_TILES
-            width = N_TILE // parts
-            for s in range(parts):
-                power = keep.tile([P, width], F32, name="power%d_%d" % (j, s))
-                nc.scalar.activation(out=power[:], in_=total[j, s][:], func=ACT.Square)
-                n0 = n * N_TILE + s * width
-                nc.sync.dma_start(out=out[m * P : (m + 1) * P, n0 : n0 + width], in_=power[:])
+        def square_and_store(j, window=whole):
+            m, n0 = j % M_TILES, j // M_TILES * N_TILE
+            power = keep.tile([P, window.stop - window.start], F32, name="power%d_%d" % (j, window.start))
+            nc.scalar.activation(out=power[:], in_=total[j][:], func=ACT.Square)
+            nc.sync.dma_start(out=out[m * P : (m + 1) * P, n0 + window.start : n0 + window.stop], in_=power[:])
 
-        turn_c()
-        copy_c()
-        sort_x(0)
-        sort_x(1)
-        sort_x(2)
+        spread_c()
+        for m in range(M_TILES - 1):
+            sort_x(m)
         turn_x(0)
         turn_x(1)
         quantize_x(0)
+        sort_x(M_TILES - 1)
         quantize_x(1)
-        turn_x(2)
-        quantize_x(2)
-        low_product(0)
-        low_product(1)
-        low_product(2)
-        sort_x(3)
-        turn_x(3)
-        quantize_x(3)
-        mid_product(0)
-        mid_product(1)
-        mid_product(2)
-        low_product(3)
-        mid_product(3)
-        for i in range(PASSES):
-            interleave_scalar(i, HEAD_SHARE)
-            interleave_vector(i, HEAD_SHARE)
-            if i > 0:
-                quantize_high(i - 1)
+        for m in range(2, M_TILES):
+            turn_x(m)
+            quantize_x(m)
+
+        for j in range(M_TILES):
+            low_product(j)
+        for j in range(M_TILES):
+            mid_product(j)
+        for piece in range(PASSES):
+            interleave_scalar(piece, HEAD_SHARE)
+            interleave_vector(piece, HEAD_SHARE)
+            if piece > 0:
+                quantize_high(piece - 1)
         quantize_high(PASSES - 1)
+
+        last = TILES - 1
         low_product(M_TILES)
         low_product(M_TILES + 1)
-
         ahead = []
-        for j in range(M_TILES, TILES):
+        for j in range(M_TILES, last):
             ahead.append((mid_product, j))
-            if j + 2 < TILES:
+            if j + 2 < last:
                 ahead.append((low_product, j + 2))
 
-        def run_ahead(count):
-            for s in range(count):
-                half, j = ahead.pop(0)
-                half(j)
-
-        piece_steps = [0,1,2,4,5,6,8,9,10]
-        counts = [2,2,1,1,2,2,1,1,2,2,1,1,1,1,1,1]
-        for j in range(TILES):
-            piece = j in piece_steps
-            i = PASSES + piece_steps.index(j) if piece else 0
+        for j in range(last):
+            m, n = j % M_TILES, j // M_TILES
+            more_columns = n + 1 < N_TILES
+            has_piece = more_columns and m < PASSES
+            piece = (n + 1) * PASSES + m
             high_product(j)
-            run_ahead(counts[j])
-            if piece:
-                interleave_scalar(i, STEADY_SHARE)
+            for ahead_product, ahead_tile in ahead[: (2 if m < 2 else 1) if more_columns else 1 - m % 2]:
+                ahead_product(ahead_tile)
+                ahead.pop(0)
+            if has_piece:
+                interleave_scalar(piece, STEADY_SHARE)
             weigh(j)
-            if piece and STEADY_SHARE:
-                interleave_vector(i, STEADY_SHARE)
-            add_up(j, 2 if j == TILES - 1 else 1)
-            if j >= 2:
-                square_and_store(j - 2, 1)
-            if piece:
-                quantize_high(i)
-        for j in range(TILES - 2, TILES):
-            square_and_store(j, 2 if j == TILES - 1 else 1)
+            if has_piece:
+                interleave_vector(piece, STEADY_SHARE)
+            add_up(j)
+            if j >= SQUARE_LAG:
+                square_and_store(j - SQUARE_LAG)
+            if has_piece:
+                quantize_high(piece)
+
+        high_product(last)
+        weigh(last)
+        for j in range(last - SQUARE_LAG, last):
+            square_and_store(j)
+        for n0 in range(0, N_TILE, P):
+            window = slice(n0, n0 + P)
+            low_product(last, window)
+            mid_product(last, window)
+            add_up(last, window)
+            square_and_store(last, window)

from contextlib import ExitStack

import concourse.mybir as mybir
from concourse.masks import make_identity

M, K, N = 512, 1536, 2048
FLOPS = 3 * 2 * M * K * N

F32 = mybir.dt.float32
BF16 = mybir.dt.bfloat16
I32 = mybir.dt.int32
U32 = mybir.dt.uint32
U8 = mybir.dt.uint8
FP8X4 = mybir.dt.float8_e4m3fn_x4
FP4X4 = mybir.dt.float4_e2m1fn_x4
ALU = mybir.AluOpType
ACT = mybir.ActivationFunctionType

P = 128
PACK = 4
K_PASS = P * PACK
PASSES = K // K_PASS
N_TILE = 512
M_TILES = M // P
N_TILES = N // N_TILE
TILES = M_TILES * N_TILES
BANKS = 8
QUADRANT = 32
SCALE_ROWS = 4
BLOCKS = K_PASS // 32
MID_ROW = 4
C_WORDS = N // P // 2
X_PARTS = ((0, 1), (1, PASSES))
HEAD_SHARE = 256
STEADY_SHARE = 144
SQUARE_LAG = 2


def tile_broadband_bartlett_power_s10_kernel(
    tc, x, low_words, low_scales, mid_words, mid_scales, high, c, out
):
    nc = tc.nc

    with ExitStack() as ctx:
        keep = ctx.enter_context(tc.tile_pool(name="keep", bufs=1))
        work = ctx.enter_context(tc.tile_pool(name="work", bufs=2))
        psum = ctx.enter_context(tc.psum_pool(name="psum", bufs=1))
        ctx.enter_context(tc.manual_schedule())

        free_banks = list(range(BANKS))

        def take_bank():
            b = free_banks.pop(0)
            return b, psum.tile([P, N_TILE], F32, name="bank%d" % b, tag="bank%d" % b)

        def cols(n):
            return slice(n * N_TILE, (n + 1) * N_TILE)

        ident = keep.tile([P, P], F32)
        make_identity(nc, ident[:])

        low_plane_first = keep.tile([P, PASSES, N_TILE], U8, align_bytes=64)
        low_plane_rest = keep.tile([P, PASSES, N - N_TILE], U8, align_bytes=64)
        mid_plane = keep.tile([P, PASSES, N], U8, align_bytes=64)
        for plane in (low_plane_first, low_plane_rest, mid_plane):
            nc.vector.memset(plane[:].bitcast(I32), 0)

        def load_scales(sources):
            for r in range(SCALE_ROWS):
                for plane, first_row, scales in sources:
                    nc.sync.dma_start(
                        out=plane[:].bitcast(I32)[first_row + r : P : QUADRANT],
                        in_=scales[:, r:BLOCKS:SCALE_ROWS, :].rearrange("g q n -> q g n").bitcast(I32),
                    )

        x_raw, low, mid, high_raw = {}, {}, {}, {}

        def load_x(m):
            x_raw[m] = keep.tile([P, K], BF16, name="x_raw%d" % m)
            nc.sync.dma_start(out=x_raw[m][:], in_=x[m * P : (m + 1) * P, :])

        def load_low(n):
            low[n] = keep.tile([P, PASSES, 2 * N_TILE], U8, name="low%d" % n, align_bytes=64)
            words = low_words.rearrange("g p b -> p g b")[:, :, 2 * n * N_TILE : 2 * (n + 1) * N_TILE]
            nc.sync.dma_start(out=low[n][:].bitcast(I32), in_=words.bitcast(I32))

        def load_mid(n):
            mid[n] = keep.tile([P, PASSES, N_TILE], U32, name="mid%d" % n, align_bytes=64)
            words = mid_words.rearrange("g p n t -> p g (n t)")[:, :, PACK * n * N_TILE : PACK * (n + 1) * N_TILE]
            nc.sync.dma_start(out=mid[n][:].bitcast(I32), in_=words.bitcast(I32))

        def load_high(n, passes):
            for g in passes:
                piece = n * PASSES + g
                high_raw[piece] = keep.tile([P, PACK, N_TILE], BF16, name="high_raw%d" % piece)
                rows = high[g * K_PASS : (g + 1) * K_PASS, cols(n)]
                nc.sync.dma_start(out=high_raw[piece][:], in_=rows.rearrange("(p t) n -> p t n", t=PACK))

        c_rows = keep.tile([P, N // P], BF16)
        nc.sync.dma_start(out=c_rows[:], in_=c.rearrange("(p i) -> p i", p=P))
        for m in range(M_TILES):
            load_x(m)
        load_low(0)
        load_scales([(low_plane_first, 0, low_scales[:, :, :N_TILE])])
        load_scales([(mid_plane, MID_ROW, mid_scales), (low_plane_rest, 0, low_scales[:, :, N_TILE:])])
        load_mid(0)
        load_high(0, range(PASSES - 1))
        load_low(1)
        load_high(0, [PASSES - 1])
        load_mid(1)
        load_high(1, range(PASSES))
        for n in range(2, N_TILES):
            load_low(n)
            load_high(n, [0])
            load_mid(n)
            load_high(n, range(1, PASSES))

        x_sorted, x_grouped, x_codes, x_scales = {}, {}, {}, {}

        def sort_x(m):
            x_sorted[m] = work.tile([P, 2, K // PACK], F32, name="x_sorted", tag="x_sorted", bufs=3)
            nc.vector.tensor_copy(
                out=x_sorted[m][:], in_=x_raw[m][:].bitcast(F32).rearrange("r (w u) -> r u w", u=2)
            )

        def turn_x(m):
            for part, (g0, g1) in enumerate(X_PARTS):
                b, bank = take_bank()
                for g in range(g0, g1):
                    for u in range(2):
                        at = (2 * (g - g0) + u) * P
                        nc.tensor.transpose(bank[:, at : at + P], x_sorted[m][:, u, P * g : P * (g + 1)], ident[:])
                width = (g1 - g0) * K_PASS
                grouped = work.tile(
                    [P, width], BF16, name="x_grouped%d" % part, tag="x_grouped%d" % part, align_bytes=64
                )
                nc.scalar.copy(
                    out=grouped[:].bitcast(F32).rearrange("p (g r u) -> p g r u", r=P, u=2),
                    in_=bank[:, : width // 2].rearrange("p (g u r) -> p g r u", r=P, u=2),
                )
                x_grouped[m, part] = grouped
                free_banks.append(b)

        def quantize_x(m):
            for part, (g0, g1) in enumerate(X_PARTS):
                width = (g1 - g0) * P
                codes = keep.tile([P, width], U32, name="x_codes%d_%d" % (m, part), align_bytes=64)
                scales = keep.tile([P, width], U8, name="x_scales%d_%d" % (m, part), align_bytes=64)
                nc.vector.quantize_mx(out=codes[:].bitcast(FP8X4), scales=scales[:], in_=x_grouped[m, part][:])
                for g in range(g0, g1):
                    x_codes[m, g] = codes[:, (g - g0) * P : (g - g0 + 1) * P]
                    x_scales[m, g] = scales[:, (g - g0) * P : (g - g0 + 1) * P]

        c_all = keep.tile([P, N], BF16)

        def spread_c():
            words = c_rows[:].bitcast(F32)
            per_bank = N_TILE // P
            taken = []
            for w0 in range(0, C_WORDS, per_bank):
                b, bank = take_bank()
                taken.append((w0, b, bank))
                for w in range(per_bank):
                    repeated = words[:, w0 + w : w0 + w + 1].to_broadcast([P, P])
                    nc.tensor.transpose(bank[:, w * P : (w + 1) * P], repeated, ident[:])
            for w0, b, bank in taken:
                nc.scalar.copy(
                    out=c_all[:].bitcast(F32).rearrange("q (p w) -> q p w", w=C_WORDS)[:, :, w0 : w0 + per_bank],
                    in_=bank[:].rearrange("q (w p) -> q p w", w=per_bank),
                )
                free_banks.append(b)

        high_grouped, high_codes, high_scales = {}, {}, {}

        def interleave(copy, piece, n0, n1):
            copy(
                out=high_grouped[piece][:, n0:n1, :],
                in_=high_raw[piece][:, :, n0:n1].rearrange("p t n -> p n t"),
            )

        def interleave_scalar(piece, share):
            high_grouped[piece] = work.tile(
                [P, N_TILE, PACK], BF16, name="high_grouped", tag="high_grouped", bufs=PASSES, align_bytes=64
            )
            interleave(nc.scalar.copy, piece, share, N_TILE)

        def interleave_vector(piece, share):
            interleave(nc.vector.tensor_copy, piece, 0, share)

        def quantize_high(piece):
            high_codes[piece] = keep.tile([P, N_TILE], U32, name="high_codes%d" % piece, align_bytes=64)
            high_scales[piece] = keep.tile([P, N_TILE], U8, name="high_scales%d" % piece, align_bytes=64)
            nc.vector.quantize_mx(
                out=high_codes[piece][:].bitcast(FP8X4),
                scales=high_scales[piece][:],
                in_=high_grouped[piece][:].rearrange("p n t -> p (n t)"),
            )

        low_mid_bank, high_bank, weighted, total = {}, {}, {}, {}
        whole = slice(0, N_TILE)

        def product(bank, j, window, codes, scales, opens, closes):
            m = j % M_TILES
            for g in range(PASSES):
                nc.tensor.matmul_mx(
                    out=bank[:, window],
                    lhsT=x_codes[m, g].bitcast(FP8X4),
                    lhsT_scale=x_scales[m, g],
                    rhs=codes[g][:, window],
                    rhs_scale=scales[g][:, window],
                    start=opens and g == 0,
                    stop=closes and g == PASSES - 1,
                )

        def low_product(j, window=whole):
            n = j // M_TILES
            low_mid_bank[j] = take_bank()
            plane, plane_cols = (low_plane_first, whole) if n == 0 else (low_plane_rest, cols(n - 1))
            codes = [low[n][:, g, :].bitcast(FP4X4) for g in range(PASSES)]
            scales = [plane[:, g, plane_cols] for g in range(PASSES)]
            product(low_mid_bank[j][1], j, window, codes, scales, True, False)

        def mid_product(j, window=whole):
            n = j // M_TILES
            codes = [mid[n][:, g, :].bitcast(FP8X4) for g in range(PASSES)]
            scales = [mid_plane[MID_ROW:P, g, cols(n)] for g in range(PASSES)]
            product(low_mid_bank[j][1], j, window, codes, scales, False, True)

        def high_product(j):
            pieces = range(j // M_TILES * PASSES, (j // M_TILES + 1) * PASSES)
            high_bank[j] = take_bank()
            codes = [high_codes[piece][:].bitcast(FP8X4) for piece in pieces]
            scales = [high_scales[piece][:] for piece in pieces]
            product(high_bank[j][1], j, whole, codes, scales, True, True)

        def weigh(j):
            b, bank = high_bank[j]
            weighted[j] = work.tile([P, N_TILE], F32, name="weighted", tag="weighted")
            nc.vector.tensor_tensor(out=weighted[j][:], in0=bank[:], in1=c_all[:, cols(j // M_TILES)], op=ALU.mult)
            free_banks.append(b)

        def add_up(j, window=whole):
            b, bank = low_mid_bank[j]
            total[j] = work.tile(
                [P, window.stop - window.start], F32, name="total", tag="total", bufs=SQUARE_LAG + 2
            )
            nc.vector.tensor_tensor(out=total[j][:], in0=bank[:, window], in1=weighted[j][:, window], op=ALU.add)
            free_banks.append(b)

        def square_and_store(j, window=whole):
            m, n0 = j % M_TILES, j // M_TILES * N_TILE
            power = keep.tile([P, window.stop - window.start], F32, name="power%d_%d" % (j, window.start))
            nc.scalar.activation(out=power[:], in_=total[j][:], func=ACT.Square)
            nc.sync.dma_start(out=out[m * P : (m + 1) * P, n0 + window.start : n0 + window.stop], in_=power[:])

        spread_c()
        for m in range(M_TILES - 1):
            sort_x(m)
        turn_x(0)
        turn_x(1)
        quantize_x(0)
        sort_x(M_TILES - 1)
        quantize_x(1)
        for m in range(2, M_TILES):
            turn_x(m)
            quantize_x(m)

        for j in range(M_TILES):
            low_product(j)
        for j in range(M_TILES):
            mid_product(j)
        for piece in range(PASSES):
            interleave_scalar(piece, HEAD_SHARE)
            interleave_vector(piece, HEAD_SHARE)
            if piece > 0:
                quantize_high(piece - 1)
        quantize_high(PASSES - 1)

        last = TILES - 1
        low_product(M_TILES)
        low_product(M_TILES + 1)
        ahead = []
        for j in range(M_TILES, last):
            ahead.append((mid_product, j))
            if j + 2 < last:
                ahead.append((low_product, j + 2))

        for j in range(last):
            m, n = j % M_TILES, j // M_TILES
            more_columns = n + 1 < N_TILES
            has_piece = more_columns and m < PASSES
            piece = (n + 1) * PASSES + m
            high_product(j)
            for ahead_product, ahead_tile in ahead[: (2 if m < 2 else 1) if more_columns else 1 - m % 2]:
                ahead_product(ahead_tile)
                ahead.pop(0)
            if has_piece:
                interleave_scalar(piece, STEADY_SHARE)
            weigh(j)
            if has_piece:
                interleave_vector(piece, STEADY_SHARE)
            add_up(j)
            if j >= SQUARE_LAG:
                square_and_store(j - SQUARE_LAG)
            if has_piece:
                quantize_high(piece)

        high_product(last)
        weigh(last)
        for j in range(last - SQUARE_LAG, last):
            square_and_store(j)
        for n0 in range(0, N_TILE, P):
            window = slice(n0, n0 + P)
            low_product(last, window)
            mid_product(last, window)
            add_up(last, window)
            square_and_store(last, window)
